import numpy as np
import ml_dtypes


def mxq(x, axis, fmt="e4m3"):
    dtype, down = {"e4m3": (ml_dtypes.float8_e4m3fn, 7), "e5m2": (ml_dtypes.float8_e5m2, 14)}[fmt]
    v = np.moveaxis(np.asarray(x, np.float32).astype(ml_dtypes.bfloat16).astype(np.float64), axis, -1)
    blocks = v.reshape(v.shape[:-1] + (-1, 32))
    amax = np.abs(blocks).max(-1, keepdims=True)
    byte = np.maximum(np.where(amax > 0, np.frexp(amax)[1] - 1 + 127, 0) - down, 1)
    scale = np.exp2(byte - 127.0)
    codes = (blocks / scale).astype(np.float32).astype(dtype).astype(np.float64)
    return np.moveaxis((codes * scale).reshape(v.shape), -1, axis)


WIDE = False


def mx_kscale(k):
    if not WIDE:
        return np.ones(k)
    levels = np.array([10, -10, 5, -5, 0])
    if k % 512:
        return np.exp2(np.random.permutation(np.resize(levels, k // 32))).repeat(32)
    a = np.empty((k // 512, 16))
    for p in range(k // 512):
        a[p, :8] = np.random.permutation(np.resize(levels, 8))
        for g in range(8):
            far = levels[np.abs(levels - a[p, g]) >= 10]
            a[p, g + 8] = far[np.random.randint(len(far))]
    return np.exp2(a.ravel()).repeat(32)


def f64(x):
    return np.asarray(x).astype(np.float64)


def striped(idx):
    return np.tile(idx.reshape(-1, 16).T, (8, 1)).astype(np.uint16)


def unstriped(offs):
    return offs[:16].T.reshape(-1).astype(np.int64)


def pack_weight(w):
    k, n = w.shape
    w = f64(np.asarray(w, np.float32).astype(ml_dtypes.bfloat16)).reshape(k // 32, 32, n)
    amax = np.abs(w).max(1)
    byte = np.clip(np.where(amax > 0, np.frexp(amax)[1] - 1 + 127 - 7, 1), 1, 254)
    scaled = (w * np.exp2(127.0 - byte)[:, None, :]).reshape(k, n).astype(np.float32)
    words = np.ascontiguousarray(scaled.reshape(k // 512, 128, 4, n).transpose(0, 1, 3, 2)).astype(ml_dtypes.float8_e4m3fn).view(np.uint8)
    return words, np.ascontiguousarray(byte.astype(np.uint8).reshape(k // 512, 16, n))


def unpack_weight(words, scales):
    g, p, n, _ = words.shape
    vals = np.ascontiguousarray(words).view(ml_dtypes.float8_e4m3fn).astype(np.float64) * np.repeat(np.exp2(scales.astype(np.float64) - 127.0), 8, axis=1)[..., None]
    return vals.transpose(0, 1, 3, 2).reshape(g * 512, n)


E2M1 = np.array([0.0, 0.5, 1.0, 1.5, 2.0, 3.0, 4.0, 6.0, -0.0, -0.5, -1.0, -1.5, -2.0, -3.0, -4.0, -6.0])


def pack_fp4(w):
    k, n = w.shape
    w = f64(np.asarray(w, np.float32).astype(ml_dtypes.bfloat16)).reshape(k // 32, 32, n)
    amax = np.abs(w).max(1)
    mant, ex = np.frexp(amax / 6.0)
    byte = np.clip(np.where(amax > 0, np.where(mant > 0.5, ex, ex - 1) + 127, 1), 1, 254)
    scaled = (w * np.exp2(127.0 - byte)[:, None, :]).reshape(k, n).astype(np.float32)
    c = np.ascontiguousarray(scaled.reshape(k // 512, 128, 4, n).transpose(0, 1, 3, 2)).astype(ml_dtypes.float4_e2m1fn).view(np.uint8) & 0xF
    words = (c[..., 0::2] | (c[..., 1::2] << 4)).reshape(k // 512, 128, 2 * n)
    return np.ascontiguousarray(words), np.ascontiguousarray(byte.astype(np.uint8).reshape(k // 512, 16, n))


def unpack_fp4(words, scales):
    g, _, n = scales.shape
    words = np.ascontiguousarray(words).reshape(g, 128, n, 2)
    nib = np.empty((g, 128, n, 4), np.uint8)
    nib[..., 0::2] = words & 0xF
    nib[..., 1::2] = words >> 4
    vals = E2M1[nib] * np.repeat(np.exp2(scales.astype(np.float64) - 127.0), 8, axis=1)[..., None]
    return vals.transpose(0, 1, 3, 2).reshape(g * 512, n)


def planes(y):
    n, m = y.shape
    v = y.astype(np.float32).astype(ml_dtypes.bfloat16).astype(np.float64).reshape(n // 32, 32, m)
    top = np.abs(v).max(1)
    byte = np.clip(np.where(top > 0, np.frexp(top)[1] - 1 + 127 - 7, 1), 1, 254)
    codes = (v * np.exp2(127.0 - byte)[:, None, :]).reshape(n, m).astype(np.float32).astype(ml_dtypes.float8_e4m3fn).view(np.uint8)
    words = codes.reshape(n // 512, 128, 4, m).transpose(0, 1, 3, 2)
    return np.ascontiguousarray(words), np.ascontiguousarray(byte.astype(np.uint8).reshape(n // 512, 16, m))


def silu(v):
    return v / (1.0 + np.exp(-np.maximum(v, -700.0)))


K, T, S, H, N = 512, 2048, 512, 512, 512


def setup_inputs():
    n = np.random.standard_normal
    s = mx_kscale(K)[:, None]
    u = mx_kscale(H)
    packed_xT = pack_weight(n((K, T)) * s)
    packed_w4 = pack_fp4(n((H, N)) / np.sqrt(H) / u[:, None])
    return {
        "x_words": packed_xT[0],
        "x_scales": packed_xT[1],
        "eT": (n((K, S)) * s).astype(np.float32),
        "w1": (n((K, H)) / np.sqrt(3 * K) / s * u).astype(np.float32),
        "w2": (n((K, H)) / np.sqrt(3 * K) / s * u).astype(np.float32),
        "w3": (n((K, H)) / np.sqrt(3 * K) / s * u).astype(np.float32),
        "w4_words": packed_w4[0],
        "w4_scales": packed_w4[1],
        "offs": striped(np.random.permutation(T)[:S]),
        "dst": striped(np.random.permutation(T)[:S]),
    }


def reference(x_words, x_scales, eT, w1, w2, w3, w4_words, w4_scales, offs, dst):
    xq = unpack_weight(x_words, x_scales)[:, unstriped(offs)]
    x_dst = unpack_weight(x_words, x_scales)[:, unstriped(dst)]
    eTq = mxq(f64(eT), 0, "e4m3")
    h = silu(mxq(f64(w1), 0, "e4m3").T @ xq + mxq(f64(w2), 0, "e4m3").T @ x_dst + mxq(f64(w3), 0, "e4m3").T @ eTq)
    out_0 = unpack_fp4(w4_words, w4_scales).T @ mxq(h, 0, "e4m3")
    return (out_0,) + planes(out_0)

@@ -1,0 +1,207 @@
+from contextlib import ExitStack
+
+import concourse.mybir as mybir
+
+K, T, S, H, N = 512, 2048, 512, 512, 512
+FLOPS = 2 * S * (3 * K * H + H * N)
+
+F32 = mybir.dt.float32
+BF16 = mybir.dt.bfloat16
+I32 = mybir.dt.int32
+U32 = mybir.dt.uint32
+U16 = mybir.dt.uint16
+U8 = mybir.dt.uint8
+FP8X4 = mybir.dt.float8_e4m3fn_x4
+FP4X4 = mybir.dt.float4_e2m1fn_x4
+SILU = mybir.ActivationFunctionType.Silu
+
+P = 128
+PACK = 4
+QUADS = 4
+CHUNK = 128
+CHUNKS = S // CHUNK
+HALF = 2
+
+
+def tile_picked_zedge_silu_po_kernel(
+    tc, x_words, x_scales, eT, w1, w2, w3, w4_words, w4_scales, offs, dst, out_0, out_1, out_2
+):
+    nc = tc.nc
+    with ExitStack() as ctx:
+        keep = ctx.enter_context(tc.tile_pool(name="keep", bufs=1))
+        psum = ctx.enter_context(tc.psum_pool(name="psum", bufs=1))
+
+        def sb(shape, dtype, name):
+            return keep.tile(shape, dtype, name=name, align_bytes=64)
+
+        def scale_rows(tile, q):
+            return tile[32 * q : 32 * q + 4, :].bitcast(I32)
+
+        offs_sb = sb([P, S // 16], U16, "offs_sb")
+        dst_sb = sb([P, S // 16], U16, "dst_sb")
+        x_table = sb([P, T], U32, "x_table")
+        xs_table = sb([P, T], U8, "xs_table")
+        w4_raw = sb([P, 2 * N], U8, "w4_raw")
+        w4s_raw = sb([P, N], U8, "w4s_raw")
+        w_raw = [sb([P, PACK, H], F32, "w_raw%d" % i) for i in range(3)]
+        e_raw = [sb([P, PACK, CHUNK], F32, "e_raw%d" % c) for c in range(CHUNKS)]
+
+        nc.vector.memset(xs_table[:].bitcast(I32), 0)
+        nc.gpsimd.memset(w4s_raw[:].bitcast(I32), 0)
+
+        def load_weight(i, w):
+            nc.sync.dma_start(w_raw[i][:], w.rearrange("(p j) c -> p j c", j=PACK))
+
+        nc.sync.dma_start(x_table[:].bitcast(I32), x_words[0].rearrange("p n t -> p (n t)").bitcast(I32))
+        nc.sync.dma_start(offs_sb[:], offs)
+        nc.sync.dma_start(dst_sb[:], dst)
+        for q in range(QUADS):
+            nc.sync.dma_start(scale_rows(xs_table, q), x_scales[0][4 * q : 4 * q + 4, :].bitcast(I32))
+        load_weight(0, w1)
+        load_weight(1, w2)
+        nc.sync.dma_start(w4_raw[:].bitcast(I32), w4_words[0].bitcast(I32))
+        for q in range(QUADS):
+            nc.sync.dma_start(scale_rows(w4s_raw, q), w4_scales[0][4 * q : 4 * q + 4, :].bitcast(I32))
+        load_weight(2, w3)
+        e_rows = eT.rearrange("(p j) n -> p j n", j=PACK)
+        for c in range(CHUNKS):
+            nc.sync.dma_start(e_raw[c][:], e_rows[:, :, c * CHUNK : (c + 1) * CHUNK])
+
+        x_codes = [sb([P, S], U32, "x_codes%d" % i) for i in range(2)]
+        x_sc = [sb([P, S], U8, "x_sc%d" % i) for i in range(2)]
+        lists = (offs_sb, dst_sb)
+        for i in range(2):
+            nc.vector.tensor_copy(x_codes[i][:], x_table[:].indirect(lists[i][:]))
+            nc.vector.tensor_copy(x_sc[i][:], xs_table[:].indirect(lists[i][:]))
+
+        w4_codes = sb([P, 2 * N], U8, "w4_codes")
+        w4_sc = sb([P, N], U8, "w4_sc")
+
+        w_bf = [[sb([P, HALF * P * PACK], BF16, "w_bf%d_%d" % (i, u)) for u in range(2)] for i in range(3)]
+        w_codes = [[sb([P, HALF * P], U32, "w_codes%d_%d" % (i, u)) for u in range(2)] for i in range(3)]
+        w_sc = [[sb([P, HALF * P], U8, "w_sc%d_%d" % (i, u)) for u in range(2)] for i in range(3)]
+
+        def cast(on_vector, out, in_):
+            if on_vector:
+                nc.vector.tensor_copy(out, in_)
+            else:
+                nc.scalar.copy(out, in_)
+
+        def round_weight(i, u, on_vector):
+            cast(
+                on_vector,
+                w_bf[i][u][:].rearrange("p (t m j) -> p m j t", t=HALF, j=PACK),
+                w_raw[i][:].rearrange("p j (m t) -> p m j t", t=PACK)[:, :, :, HALF * u : HALF * u + HALF],
+            )
+
+        def quantize(codes, scales, values):
+            nc.vector.quantize_mx(out=codes.bitcast(FP8X4), scales=scales, in_=values)
+
+        def quantize_weight(i, u):
+            quantize(w_codes[i][u][:], w_sc[i][u][:], w_bf[i][u][:])
+
+        h_bank = [psum.tile([P, PACK * CHUNK], F32, name="h_bank%d" % c) for c in range(CHUNKS)]
+        o_bank = [psum.tile([P, PACK * CHUNK], F32, name="o_bank%d" % c) for c in range(CHUNKS)]
+
+        def first_layer(i, c, codes, scales):
+            for t in range(PACK):
+                cols = slice((t % HALF) * P, (t % HALF + 1) * P)
+                nc.tensor.matmul_mx(
+                    out=h_bank[c][:, t * CHUNK : (t + 1) * CHUNK],
+                    lhsT=w_codes[i][t // HALF][:, cols].bitcast(FP8X4),
+                    lhsT_scale=w_sc[i][t // HALF][:, cols],
+                    rhs=codes.bitcast(FP8X4),
+                    rhs_scale=scales,
+                    start=(i == 0 and t == 0),
+                    stop=(i == 2 and t == PACK - 1),
+                )
+
+        def interleave(on_vector, out, in_):
+            cast(
+                on_vector,
+                out[:].rearrange("p (c i j) -> p c j i", i=4, j=PACK),
+                in_[:].rearrange("p j (c i) -> p c j i", i=4),
+            )
+
+        e_bf = [sb([P, PACK * CHUNK], BF16, "e_bf%d" % c) for c in range(CHUNKS)]
+        e_codes = [sb([P, CHUNK], U32, "e_codes%d" % c) for c in range(CHUNKS)]
+        e_sc = [sb([P, CHUNK], U8, "e_sc%d" % c) for c in range(CHUNKS)]
+        h_bf = [sb([P, PACK * CHUNK], BF16, "h_bf%d" % c) for c in range(CHUNKS)]
+        h_codes = [sb([P, CHUNK], U32, "h_codes%d" % c) for c in range(CHUNKS)]
+        h_sc = [sb([P, CHUNK], U8, "h_sc%d" % c) for c in range(CHUNKS)]
+        o_f32 = [sb([P, PACK, CHUNK], F32, "o_f32_%d" % c) for c in range(CHUNKS)]
+        o_bf = [sb([P, PACK * CHUNK], BF16, "o_bf%d" % c) for c in range(CHUNKS)]
+        o_codes = sb([P, S], U32, "o_codes")
+        o_sc = sb([P, S], U8, "o_sc")
+
+        for i in range(2):
+            round_weight(i, 0, on_vector=(i == 1))
+            round_weight(i, 1, on_vector=False)
+            quantize_weight(i, 0)
+            quantize_weight(i, 1)
+            for c in range(CHUNKS):
+                cols = slice(c * CHUNK, (c + 1) * CHUNK)
+                first_layer(i, c, x_codes[i][:, cols], x_sc[i][:, cols])
+        nc.scalar.copy(
+            w4_codes[:].bitcast(U16).rearrange("p (t m) -> p t m", t=PACK),
+            w4_raw[:].bitcast(U16).rearrange("p (m t) -> p t m", t=PACK),
+        )
+        nc.vector.tensor_copy(
+            w4_sc[:].rearrange("p (t m) -> p t m", t=PACK),
+            w4s_raw[:].rearrange("p (m t) -> p t m", t=PACK),
+        )
+
+        round_weight(2, 0, on_vector=True)
+        round_weight(2, 1, on_vector=False)
+        interleave(True, e_bf[0], e_raw[0])
+        quantize_weight(2, 0)
+        quantize_weight(2, 1)
+
+        out_rows = out_0.rearrange("(p t) n -> p t n", t=PACK)
+        out_words = out_1[0].rearrange("p n t -> p (n t)").bitcast(I32)
+
+        def stage_edges(c):
+            if c > 0:
+                interleave(c == CHUNKS - 1, e_bf[c], e_raw[c])
+            quantize(e_codes[c][:], e_sc[c][:], e_bf[c][:])
+            first_layer(2, c, e_codes[c][:], e_sc[c][:])
+
+        def stage_hidden(c):
+            nc.scalar.activation(
+                h_bf[c][:].rearrange("p (n t) -> p n t", t=PACK),
+                h_bank[c][:].rearrange("p (t n) -> p n t", t=PACK),
+                SILU,
+            )
+            quantize(h_codes[c][:], h_sc[c][:], h_bf[c][:])
+            for t in range(PACK):
+                nc.tensor.matmul_mx(
+                    out=o_bank[c][:, t * CHUNK : (t + 1) * CHUNK],
+                    lhsT=w4_codes[:, 2 * P * t : 2 * P * (t + 1)].bitcast(FP4X4),
+                    lhsT_scale=w4_sc[:, P * t : P * (t + 1)],
+                    rhs=h_codes[c][:].bitcast(FP8X4),
+                    rhs_scale=h_sc[c][:],
+                    start=True,
+                    stop=True,
+                )
+
+        def stage_out(c):
+            cols = slice(c * CHUNK, (c + 1) * CHUNK)
+            cast(c == 0, o_f32[c][:].rearrange("p t n -> p (t n)"), o_bank[c][:])
+            nc.sync.dma_start(out_rows[:, :, cols], o_f32[c][:])
+            interleave(True, o_bf[c], o_f32[c])
+            quantize(o_codes[:, cols], o_sc[:, cols], o_bf[c][:])
+
+        for c in range(CHUNKS):
+            stage_edges(c)
+        for c in range(CHUNKS):
+            stage_hidden(c)
+        for c in range(CHUNKS):
+            stage_out(c)
+            if c == CHUNKS - 2:
+                early = slice(0, S - CHUNK)
+                nc.sync.dma_start(out_words[:, early], o_codes[:, early].bitcast(I32))
+        last = slice(S - CHUNK, S)
+        nc.sync.dma_start(out_words[:, last], o_codes[:, last].bitcast(I32))
+        for q in range(QUADS):
+            queue = nc.scalar if q % 2 == 0 else nc.sync
+            queue.dma_start(out_2[0][4 * q : 4 * q + 4, :].bitcast(I32), scale_rows(o_sc, q))

@@ -46,6 +46,10 @@ def tile_picked_zedge_silu_po_kernel(
         w_raw = [sb([P, PACK, H], F32, "w_raw%d" % i) for i in range(3)]
         e_raw = [sb([P, PACK, CHUNK], F32, "e_raw%d" % c) for c in range(CHUNKS)]
 
+        warm = sb([P, 1], F32, "warm")
+        warm_out = sb([P, 1], F32, "warm_out")
+        nc.gpsimd.memset(warm[:], 0.0)
+        nc.scalar.activation(warm_out[:], warm[:], SILU)
         nc.vector.memset(xs_table[:].bitcast(I32), 0)
         nc.gpsimd.memset(w4s_raw[:].bitcast(I32), 0)
 

@@ -35,7 +35,7 @@ def tile_picked_zedge_silu_po_kernel(
             return keep.tile(shape, dtype, name=name, align_bytes=64)
 
         def scale_rows(tile, q):
-            return tile[32 * q : 32 * q + 4, :].bitcast(I32)
+            return tile[q:P:32, :].bitcast(I32)
 
         offs_sb = sb([P, S // 16], U16, "offs_sb")
         dst_sb = sb([P, S // 16], U16, "dst_sb")
@@ -60,12 +60,12 @@ def tile_picked_zedge_silu_po_kernel(
         nc.sync.dma_start(offs_sb[:], offs)
         nc.sync.dma_start(dst_sb[:], dst)
         for q in range(QUADS):
-            nc.sync.dma_start(scale_rows(xs_table, q), x_scales[0][4 * q : 4 * q + 4, :].bitcast(I32))
+            nc.sync.dma_start(scale_rows(xs_table, q), x_scales[0][q:16:4, :].bitcast(I32))
         load_weight(0, w1)
         load_weight(1, w2)
         nc.sync.dma_start(w4_raw[:].bitcast(I32), w4_words[0].bitcast(I32))
         for q in range(QUADS):
-            nc.sync.dma_start(scale_rows(w4s_raw, q), w4_scales[0][4 * q : 4 * q + 4, :].bitcast(I32))
+            nc.sync.dma_start(scale_rows(w4s_raw, q), w4_scales[0][q:16:4, :].bitcast(I32))
         load_weight(2, w3)
         e_rows = eT.rearrange("(p j) n -> p j n", j=PACK)
         for c in range(CHUNKS):
@@ -208,4 +208,4 @@ def tile_picked_zedge_silu_po_kernel(
         nc.sync.dma_start(out_words[:, last], o_codes[:, last].bitcast(I32))
         for q in range(QUADS):
             queue = nc.scalar if q % 2 == 0 else nc.sync
-            queue.dma_start(out_2[0][4 * q : 4 * q + 4, :].bitcast(I32), scale_rows(o_sc, q))
+            queue.dma_start(out_2[0][q:16:4, :].bitcast(I32), scale_rows(o_sc, q))

@@ -159,6 +159,7 @@ def tile_picked_zedge_silu_po_kernel(
         round_weight(2, 1, on_vector=False)
         interleave(True, e_bf[0], e_raw[0])
         quantize_weight(2, 0)
+        quantize(e_codes[0][:], e_sc[0][:], e_bf[0][:])
         quantize_weight(2, 1)
 
         out_rows = out_0.rearrange("(p t) n -> p t n", t=PACK)
@@ -166,8 +167,8 @@ def tile_picked_zedge_silu_po_kernel(
 
         def stage_edges(c):
             if c > 0:
-                interleave(c == CHUNKS - 1, e_bf[c], e_raw[c])
-            quantize(e_codes[c][:], e_sc[c][:], e_bf[c][:])
+                interleave(c >= 2, e_bf[c], e_raw[c])
+                quantize(e_codes[c][:], e_sc[c][:], e_bf[c][:])
             first_layer(2, c, e_codes[c][:], e_sc[c][:])
 
         def stage_hidden(c):

from contextlib import ExitStack

import concourse.mybir as mybir

K, T, S, H, N = 512, 2048, 512, 512, 512
FLOPS = 2 * S * (3 * K * H + H * N)

F32 = mybir.dt.float32
BF16 = mybir.dt.bfloat16
I32 = mybir.dt.int32
U32 = mybir.dt.uint32
U16 = mybir.dt.uint16
U8 = mybir.dt.uint8
FP8X4 = mybir.dt.float8_e4m3fn_x4
FP4X4 = mybir.dt.float4_e2m1fn_x4
SILU = mybir.ActivationFunctionType.Silu

P = 128
PACK = 4
QUADS = 4
CHUNK = 128
CHUNKS = S // CHUNK
HALF = 2


def tile_picked_zedge_silu_po_kernel(
    tc, x_words, x_scales, eT, w1, w2, w3, w4_words, w4_scales, offs, dst, out_0, out_1, out_2
):
    nc = tc.nc
    with ExitStack() as ctx:
        keep = ctx.enter_context(tc.tile_pool(name="keep", bufs=1))
        psum = ctx.enter_context(tc.psum_pool(name="psum", bufs=1))

        def sb(shape, dtype, name):
            return keep.tile(shape, dtype, name=name, align_bytes=64)

        def scale_rows(tile, q):
            return tile[q:P:32, :].bitcast(I32)

        offs_sb = sb([P, S // 16], U16, "offs_sb")
        dst_sb = sb([P, S // 16], U16, "dst_sb")
        x_table = sb([P, T], U32, "x_table")
        xs_table = sb([P, T], U8, "xs_table")
        w4_raw = sb([P, 2 * N], U8, "w4_raw")
        w4s_raw = sb([P, N], U8, "w4s_raw")
        w_raw = [sb([P, PACK, H], F32, "w_raw%d" % i) for i in range(3)]
        e_raw = [sb([P, PACK, CHUNK], F32, "e_raw%d" % c) for c in range(CHUNKS)]

        warm = sb([P, 1], F32, "warm")
        warm_out = sb([P, 1], F32, "warm_out")
        nc.gpsimd.memset(warm[:], 0.0)
        nc.scalar.activation(warm_out[:], warm[:], SILU)
        nc.vector.memset(xs_table[:].bitcast(I32), 0)
        nc.gpsimd.memset(w4s_raw[:].bitcast(I32), 0)

        def load_weight(i, w):
            nc.sync.dma_start(w_raw[i][:], w.rearrange("(p j) c -> p j c", j=PACK))

        nc.sync.dma_start(x_table[:].bitcast(I32), x_words[0].rearrange("p n t -> p (n t)").bitcast(I32))
        nc.sync.dma_start(offs_sb[:], offs)
        nc.sync.dma_start(dst_sb[:], dst)
        for q in range(QUADS):
            nc.sync.dma_start(scale_rows(xs_table, q), x_scales[0][q:16:4, :].bitcast(I32))
        load_weight(0, w1)
        load_weight(1, w2)
        nc.sync.dma_start(w4_raw[:].bitcast(I32), w4_words[0].bitcast(I32))
        for q in range(QUADS):
            nc.sync.dma_start(scale_rows(w4s_raw, q), w4_scales[0][q:16:4, :].bitcast(I32))
        load_weight(2, w3)
        e_rows = eT.rearrange("(p j) n -> p j n", j=PACK)
        for c in range(CHUNKS):
            nc.sync.dma_start(e_raw[c][:], e_rows[:, :, c * CHUNK : (c + 1) * CHUNK])

        x_codes = [sb([P, S], U32, "x_codes%d" % i) for i in range(2)]
        x_sc = [sb([P, S], U8, "x_sc%d" % i) for i in range(2)]
        lists = (offs_sb, dst_sb)
        for i in range(2):
            nc.vector.tensor_copy(x_codes[i][:], x_table[:].indirect(lists[i][:]))
            nc.vector.tensor_copy(x_sc[i][:], xs_table[:].indirect(lists[i][:]))

        w4_codes = sb([P, 2 * N], U8, "w4_codes")
        w4_sc = sb([P, N], U8, "w4_sc")

        w_bf = [[sb([P, HALF * P * PACK], BF16, "w_bf%d_%d" % (i, u)) for u in range(2)] for i in range(3)]
        w_codes = [[sb([P, HALF * P], U32, "w_codes%d_%d" % (i, u)) for u in range(2)] for i in range(3)]
        w_sc = [[sb([P, HALF * P], U8, "w_sc%d_%d" % (i, u)) for u in range(2)] for i in range(3)]

        def cast(on_vector, out, in_):
            if on_vector:
                nc.vector.tensor_copy(out, in_)
            else:
                nc.scalar.copy(out, in_)

        def round_weight(i, u, on_vector):
            cast(
                on_vector,
                w_bf[i][u][:].rearrange("p (t m j) -> p m j t", t=HALF, j=PACK),
                w_raw[i][:].rearrange("p j (m t) -> p m j t", t=PACK)[:, :, :, HALF * u : HALF * u + HALF],
            )

        def quantize(codes, scales, values):
            nc.vector.quantize_mx(out=codes.bitcast(FP8X4), scales=scales, in_=values)

        def quantize_weight(i, u):
            quantize(w_codes[i][u][:], w_sc[i][u][:], w_bf[i][u][:])

        h_bank = [psum.tile([P, PACK * CHUNK], F32, name="h_bank%d" % c) for c in range(CHUNKS)]
        o_bank = [psum.tile([P, PACK * CHUNK], F32, name="o_bank%d" % c) for c in range(CHUNKS)]

        def first_layer(i, c, codes, scales):
            for t in range(PACK):
                cols = slice((t % HALF) * P, (t % HALF + 1) * P)
                nc.tensor.matmul_mx(
                    out=h_bank[c][:, t * CHUNK : (t + 1) * CHUNK],
                    lhsT=w_codes[i][t // HALF][:, cols].bitcast(FP8X4),
                    lhsT_scale=w_sc[i][t // HALF][:, cols],
                    rhs=codes.bitcast(FP8X4),
                    rhs_scale=scales,
                    start=(i == 0 and t == 0),
                    stop=(i == 2 and t == PACK - 1),
                )

        def interleave(on_vector, out, in_):
            cast(
                on_vector,
                out[:].rearrange("p (c i j) -> p c j i", i=4, j=PACK),
                in_[:].rearrange("p j (c i) -> p c j i", i=4),
            )

        e_bf = [sb([P, PACK * CHUNK], BF16, "e_bf%d" % c) for c in range(CHUNKS)]
        e_codes = [sb([P, CHUNK], U32, "e_codes%d" % c) for c in range(CHUNKS)]
        e_sc = [sb([P, CHUNK], U8, "e_sc%d" % c) for c in range(CHUNKS)]
        h_bf = [sb([P, PACK * CHUNK], BF16, "h_bf%d" % c) for c in range(CHUNKS)]
        h_codes = [sb([P, CHUNK], U32, "h_codes%d" % c) for c in range(CHUNKS)]
        h_sc = [sb([P, CHUNK], U8, "h_sc%d" % c) for c in range(CHUNKS)]
        o_f32 = [sb([P, PACK, CHUNK], F32, "o_f32_%d" % c) for c in range(CHUNKS)]
        o_bf = [sb([P, PACK * CHUNK], BF16, "o_bf%d" % c) for c in range(CHUNKS)]
        o_codes = sb([P, S], U32, "o_codes")
        o_sc = sb([P, S], U8, "o_sc")

        for i in range(2):
            round_weight(i, 0, on_vector=(i == 1))
            round_weight(i, 1, on_vector=False)
            quantize_weight(i, 0)
            quantize_weight(i, 1)
            for c in range(CHUNKS):
                cols = slice(c * CHUNK, (c + 1) * CHUNK)
                first_layer(i, c, x_codes[i][:, cols], x_sc[i][:, cols])
        nc.scalar.copy(
            w4_codes[:].bitcast(U16).rearrange("p (t m) -> p t m", t=PACK),
            w4_raw[:].bitcast(U16).rearrange("p (m t) -> p t m", t=PACK),
        )
        nc.vector.tensor_copy(
            w4_sc[:].rearrange("p (t m) -> p t m", t=PACK),
            w4s_raw[:].rearrange("p (m t) -> p t m", t=PACK),
        )

        round_weight(2, 0, on_vector=True)
        round_weight(2, 1, on_vector=False)
        interleave(True, e_bf[0], e_raw[0])
        quantize_weight(2, 0)
        quantize(e_codes[0][:], e_sc[0][:], e_bf[0][:])
        quantize_weight(2, 1)

        out_rows = out_0.rearrange("(p t) n -> p t n", t=PACK)
        out_words = out_1[0].rearrange("p n t -> p (n t)").bitcast(I32)

        def stage_edges(c):
            if c > 0:
                interleave(c >= 2, e_bf[c], e_raw[c])
                quantize(e_codes[c][:], e_sc[c][:], e_bf[c][:])
            first_layer(2, c, e_codes[c][:], e_sc[c][:])

        def stage_hidden(c):
            nc.scalar.activation(
                h_bf[c][:].rearrange("p (n t) -> p n t", t=PACK),
                h_bank[c][:].rearrange("p (t n) -> p n t", t=PACK),
                SILU,
            )
            quantize(h_codes[c][:], h_sc[c][:], h_bf[c][:])
            for t in range(PACK):
                nc.tensor.matmul_mx(
                    out=o_bank[c][:, t * CHUNK : (t + 1) * CHUNK],
                    lhsT=w4_codes[:, 2 * P * t : 2 * P * (t + 1)].bitcast(FP4X4),
                    lhsT_scale=w4_sc[:, P * t : P * (t + 1)],
                    rhs=h_codes[c][:].bitcast(FP8X4),
                    rhs_scale=h_sc[c][:],
                    start=True,
                    stop=True,
                )

        def stage_out(c):
            cols = slice(c * CHUNK, (c + 1) * CHUNK)
            cast(c == 0, o_f32[c][:].rearrange("p t n -> p (t n)"), o_bank[c][:])
            nc.sync.dma_start(out_rows[:, :, cols], o_f32[c][:])
            interleave(True, o_bf[c], o_f32[c])
            quantize(o_codes[:, cols], o_sc[:, cols], o_bf[c][:])

        for c in range(CHUNKS):
            stage_edges(c)
        for c in range(CHUNKS):
            stage_hidden(c)
        for c in range(CHUNKS):
            stage_out(c)
            if c == CHUNKS - 2:
                early = slice(0, S - CHUNK)
                nc.sync.dma_start(out_words[:, early], o_codes[:, early].bitcast(I32))
        last = slice(S - CHUNK, S)
        nc.sync.dma_start(out_words[:, last], o_codes[:, last].bitcast(I32))
        for q in range(QUADS):
            queue = nc.scalar if q % 2 == 0 else nc.sync
            queue.dma_start(out_2[0][q:16:4, :].bitcast(I32), scale_rows(o_sc, q))
